import numpy as np
import ml_dtypes


def mxq(x, axis, fmt="e4m3"):
    dtype, down = {"e4m3": (ml_dtypes.float8_e4m3fn, 7), "e5m2": (ml_dtypes.float8_e5m2, 14)}[fmt]
    v = np.moveaxis(np.asarray(x, np.float32).astype(ml_dtypes.bfloat16).astype(np.float64), axis, -1)
    blocks = v.reshape(v.shape[:-1] + (-1, 32))
    amax = np.abs(blocks).max(-1, keepdims=True)
    byte = np.maximum(np.where(amax > 0, np.frexp(amax)[1] - 1 + 127, 0) - down, 1)
    scale = np.exp2(byte - 127.0)
    codes = (blocks / scale).astype(np.float32).astype(dtype).astype(np.float64)
    return np.moveaxis((codes * scale).reshape(v.shape), -1, axis)


WIDE = False


def mx_kscale(k):
    if not WIDE:
        return np.ones(k)
    levels = np.array([10, -10, 5, -5, 0])
    if k % 512:
        return np.exp2(np.random.permutation(np.resize(levels, k // 32))).repeat(32)
    a = np.empty((k // 512, 16))
    for p in range(k // 512):
        a[p, :8] = np.random.permutation(np.resize(levels, 8))
        for g in range(8):
            far = levels[np.abs(levels - a[p, g]) >= 10]
            a[p, g + 8] = far[np.random.randint(len(far))]
    return np.exp2(a.ravel()).repeat(32)


def f64(x):
    return np.asarray(x).astype(np.float64)


def striped(idx):
    return np.tile(idx.reshape(-1, 16).T, (8, 1)).astype(np.uint16)


def unstriped(offs):
    return offs[:16].T.reshape(-1).astype(np.int64)


E2M1 = np.array([0.0, 0.5, 1.0, 1.5, 2.0, 3.0, 4.0, 6.0, -0.0, -0.5, -1.0, -1.5, -2.0, -3.0, -4.0, -6.0])


def pack_weight(w, fmt):
    k, n = w.shape
    w = f64(np.asarray(w, np.float32).astype(ml_dtypes.bfloat16)).reshape(k // 32, 32, n)
    amax = np.abs(w).max(1)
    if fmt == "e4m3":
        byte = np.frexp(amax)[1] - 1 + 127 - 7
    else:
        mant, ex = np.frexp(amax / 6.0)
        byte = np.where(mant > 0.5, ex, ex - 1) + 127
    byte = np.clip(np.where(amax > 0, byte, 1), 1, 254)
    scaled = (w * np.exp2(127.0 - byte)[:, None, :]).reshape(k, n).astype(np.float32)
    by_word = np.ascontiguousarray(scaled.reshape(k // 512, 128, 4, n).transpose(0, 1, 3, 2))
    if fmt == "e4m3":
        words = by_word.astype(ml_dtypes.float8_e4m3fn).view(np.uint8)
    else:
        c = by_word.astype(ml_dtypes.float4_e2m1fn).view(np.uint8) & 0xF
        words = (c[..., 0::2] | (c[..., 1::2] << 4)).reshape(k // 512, 128, 2 * n)
    return np.ascontiguousarray(words), np.ascontiguousarray(byte.astype(np.uint8).reshape(k // 512, 16, n))


def unpack_weight(words, scales, fmt):
    g, _, n = scales.shape
    words = np.ascontiguousarray(words).reshape(g, 128, n, -1)
    if fmt == "e4m3":
        vals = words.view(ml_dtypes.float8_e4m3fn).astype(np.float64)
    else:
        nib = np.empty((g, 128, n, 4), np.uint8)
        nib[..., 0::2] = words & 0xF
        nib[..., 1::2] = words >> 4
        vals = E2M1[nib]
    vals = vals * np.repeat(np.exp2(scales.astype(np.float64) - 127.0), 8, axis=1)[..., None]
    return vals.transpose(0, 1, 3, 2).reshape(g * 512, n)


def gelu(v):
    return 0.5 * v * (1.0 + np.tanh(np.sqrt(2.0 / np.pi) * (v + 0.044715 * v**3)))


K, T, S, H, T2, P = 1536, 4096, 1024, 512, 2048, 1024

def setup_inputs():
    n = np.random.standard_normal
    s = mx_kscale(K)[:, None]
    u = mx_kscale(H)[:, None]
    d = {}
    d["tab_words"], d["tab_scales"] = pack_weight(n((K, T)) * s, "e4m3")
    d["offs"] = striped(np.random.permutation(T)[:S])
    d["offs2"] = striped(np.random.permutation(T2)[:S])
    d["offs3"] = striped(np.random.permutation(T2)[:P])
    d["offs4"] = striped(np.random.permutation(T2)[:P])
    d["w1"] = (n((K, H)) * 1.5 / K ** 0.5 / s).astype(np.float32)
    d["gain"] = (1.3 * np.exp(0.3 * n(H)) * u[:, 0]).astype(np.float32)
    d["wgs"] = np.exp(0.3 * n((128, S))).astype(np.float32)
    d["page0"] = (n((H, T2)) * u).astype(np.float32)
    d["wear"] = (0.7 * n(H) * u[:, 0]).astype(np.float32)
    d["w4_words"], d["w4_scales"] = pack_weight(n((H, H)) * 1.2 / H ** 0.5 / u, "e2m1")
    d["w3"] = (n((H, H)) / H ** 0.5 / u / u.T).astype(np.float32)
    d["wgo"] = np.exp(0.3 * n((128, P))).astype(np.float32)
    d["page1"] = n((H, T2)).astype(np.float32)
    return d

def reference(tab_words, tab_scales, offs, offs2, offs3, offs4, w1, gain, wgs, page0, wear,
              w4_words, w4_scales, w3, wgo, page1):
    v = unpack_weight(tab_words, tab_scales, "e4m3")[:, unstriped(offs)]
    w4 = unpack_weight(w4_words, w4_scales, "e2m1")
    h = np.tanh(mxq(f64(w1), 0, "e4m3").T @ v) * f64(gain)[:, None]
    page = f64(page0).copy()
    page[:, unstriped(offs2)] = np.tile(f64(wgs), (H // 128, 1)) * h
    die = page[:, unstriped(offs3)]
    x = mxq(die + f64(wear)[:, None], 0, "e4m3")
    a = w4.T @ x
    b = mxq(f64(w3), 0, "e4m3").T @ x
    y = a / (1.0 + np.exp(-a)) + b * die
    out = f64(page1).copy()
    out[:, unstriped(offs4)] = np.tile(f64(wgo), (H // 128, 1)) * y
    return out

@@ -1,0 +1,258 @@
+from contextlib import ExitStack
+
+import concourse.mybir as mybir
+from concourse.masks import make_identity
+
+K, T, S, H, T2, NP = 1536, 4096, 1024, 512, 2048, 1024
+FLOPS = 2 * K * H * S + 2 * 2 * H * H * NP
+
+F32 = mybir.dt.float32
+BF16 = mybir.dt.bfloat16
+I32 = mybir.dt.int32
+U32 = mybir.dt.uint32
+U16 = mybir.dt.uint16
+U8 = mybir.dt.uint8
+FP8X4 = mybir.dt.float8_e4m3fn_x4
+FP4X4 = mybir.dt.float4_e2m1fn_x4
+ACT = mybir.ActivationFunctionType
+MULT = mybir.AluOpType.mult
+ADD = mybir.AluOpType.add
+
+P = 128
+PASSES = K // 512
+ROWT = H // P
+HALF = 512
+CH = 256
+WCOL = 256
+
+
+def tile_list_coin_die_catalogue_kernel(
+    tc, tab_words, tab_scales, offs, offs2, offs3, offs4, w1, gain, wgs, page0, wear,
+    w4_words, w4_scales, w3, wgo, page1, out,
+):
+    nc = tc.nc
+    with ExitStack() as ctx:
+        lists = ctx.enter_context(tc.tile_pool(name="lists", bufs=1))
+        keep = ctx.enter_context(tc.tile_pool(name="keep", bufs=1))
+        psum = ctx.enter_context(tc.psum_pool(name="psum", bufs=1))
+
+        def load_list(src, name):
+            tile = lists.tile([P, src.shape[1]], U16, name=name)
+            nc.sync.dma_start(tile[:], src)
+            return tile
+
+        def entries(tile, start, count):
+            return tile[:, start // 16 : (start + count) // 16]
+
+        scale_win = keep.tile([P, T], U8, name="scale_win")
+        nc.vector.memset(scale_win[:].bitcast(I32), 0)
+        w4_plane = keep.tile([P, H], U8, name="w4_plane", align_bytes=64)
+        nc.vector.memset(w4_plane[:].bitcast(I32), 0)
+        vec_rows = keep.tile([P, P], F32, name="vec_rows")
+        nc.gpsimd.memset(vec_rows[:], 0.0)
+        ident = keep.tile([P, P], F32, name="ident")
+        make_identity(nc, ident[:])
+        ident_bf = keep.tile([P, P], BF16, name="ident_bf")
+        make_identity(nc, ident_bf[:])
+
+        def load_words(a):
+            tile = keep.tile([P, T], U32, name="words%d" % a, tag="big", bufs=PASSES)
+            nc.sync.dma_start(tile[:].bitcast(I32), tab_words[a].rearrange("p t i -> p (t i)").bitcast(I32))
+            return tile
+
+        def load_w1(g):
+            tiles = []
+            for a in range(PASSES):
+                raw = keep.tile([P, 4, WCOL], F32, name="w1_raw%d_%d" % (g, a), tag="w1_raw", bufs=PASSES)
+                rows = w1[512 * a : 512 * (a + 1), WCOL * g : WCOL * (g + 1)]
+                nc.sync.dma_start(raw[:], rows.rearrange("(p i) c -> p i c", i=4))
+                tiles.append(raw)
+            return tiles
+
+        def load_page(src, u, name):
+            tile = keep.tile([P, T2], F32, name="%s_%d" % (name, u))
+            nc.sync.dma_start(tile[:], src[P * u : P * (u + 1), :])
+            return tile
+
+        def quantise_weight(raw, name, tag, bufs):
+            width = raw.shape[2]
+            grouped = keep.tile([P, width, 4], BF16, name=name + "_bf", tag=tag, bufs=bufs, align_bytes=64)
+            nc.scalar.copy(
+                out=grouped[:].rearrange("p (c n) i -> p c i n", n=4),
+                in_=raw[:].rearrange("p i (c n) -> p c i n", n=4),
+            )
+            codes = keep.tile([P, width], U32, name=name + "_codes", align_bytes=64)
+            plane = keep.tile([P, width], U8, name=name + "_plane", align_bytes=64)
+            nc.vector.quantize_mx(
+                out=codes[:].bitcast(FP8X4), scales=plane[:], in_=grouped[:].rearrange("p c i -> p (c i)")
+            )
+            return codes, plane
+
+        words = [load_words(0)]
+        idx = load_list(offs, "idx")
+        for q in range(4):
+            nc.scalar.dma_start(
+                scale_win[32 * q : 32 * q + 4 * PASSES, :].bitcast(I32),
+                tab_scales[:, 4 * q : 4 * q + 4, :].bitcast(I32),
+            )
+        nc.scalar.dma_start(vec_rows[0:ROWT, :], gain.rearrange("(u p) -> u p", p=P))
+        nc.scalar.dma_start(vec_rows[ROWT : 2 * ROWT, :], wear.rearrange("(u p) -> u p", p=P))
+        words.append(load_words(1))
+        w1_raw = [load_w1(0)]
+        words.append(load_words(2))
+        idx2 = load_list(offs2, "idx2")
+        wgs_sb = keep.tile([P, S], F32, name="wgs_sb")
+        nc.sync.dma_start(wgs_sb[:], wgs)
+        cache = [load_page(page0, 0, "cache")]
+
+        vec_ps = psum.tile([P, P], F32, name="vec_ps", tag="turn2", bufs=2)
+        nc.tensor.transpose(vec_ps[:], vec_rows[:], ident[:])
+        cols = keep.tile([P, 2 * ROWT], F32, name="cols")
+        nc.scalar.copy(out=cols[:], in_=vec_ps[:, 0 : 2 * ROWT])
+
+        v_words = [keep.tile([P, S], U32, name="v_words%d" % a, align_bytes=64) for a in range(PASSES)]
+        v_plane = keep.tile([P, S], U8, name="v_plane", align_bytes=64)
+        nc.vector.tensor_copy(v_words[0][:], words[0][:].indirect(idx[:]))
+        nc.vector.tensor_copy(v_plane[:], scale_win[:].indirect(idx[:]))
+        nc.vector.tensor_copy(v_words[1][:], words[1][:].indirect(idx[:]))
+        w1_q = [[quantise_weight(w1_raw[0][a], "w1_0_%d" % a, "w1_bf", PASSES) for a in range(PASSES)]]
+        for hh in range(2):
+            nc.vector.tensor_copy(
+                v_words[2][:, HALF * hh : HALF * (hh + 1)], words[2][:].indirect(entries(idx, HALF * hh, HALF))
+            )
+
+        h = keep.tile([P, ROWT, S], F32, name="h", tag="state")
+
+        def first_stage(u):
+            g, m0 = divmod(P * u, WCOL)
+            for hh in range(2):
+                js = slice(HALF * hh, HALF * (hh + 1))
+                acc = psum.tile([P, HALF], F32, name="acc", tag="acc", bufs=4)
+                for a in range(PASSES):
+                    codes, plane = w1_q[g][a]
+                    nc.tensor.matmul_mx(
+                        out=acc[:],
+                        lhsT=codes[:, m0 : m0 + P].bitcast(FP8X4),
+                        lhsT_scale=plane[:, m0 : m0 + P],
+                        rhs=v_words[a][:, js].bitcast(FP8X4),
+                        rhs_scale=v_plane[4 * a : P, js],
+                        start=(a == 0),
+                        stop=(a == PASSES - 1),
+                    )
+                nc.scalar.activation(out=h[:, u, js], in_=acc[:], func=ACT.Tanh)
+                nc.scalar.activation(out=h[:, u, js], in_=h[:, u, js], func=ACT.Copy, scale=cols[:, u : u + 1])
+
+        def put_state(u, start, count):
+            js = slice(start, start + count)
+            nc.vector.tensor_tensor(
+                cache[u][:].indirect(entries(idx2, start, count)), h[:, u, js], wgs_sb[:, js], MULT
+            )
+
+        first_stage(0)
+        put_state(0, 0, HALF)
+        put_state(0, HALF, HALF)
+        first_stage(1)
+
+        w1_raw.append(load_w1(1))
+        wgo_sb = keep.tile([P, NP], F32, name="wgo_sb")
+        nc.sync.dma_start(wgo_sb[:], wgo)
+        cache.append(load_page(page0, 1, "cache"))
+        cache.append(load_page(page0, 2, "cache"))
+        w3_raw = keep.tile([P, 4, H], F32, name="w3_raw")
+        nc.sync.dma_start(w3_raw[:], w3.rearrange("(p i) c -> p i c", i=4))
+        idx3 = load_list(offs3, "idx3")
+        w4_codes = keep.tile([P, 2 * H], U8, name="w4_codes", align_bytes=64)
+        nc.sync.dma_start(w4_codes[:].bitcast(I32), w4_words[0].bitcast(I32))
+        for q in range(4):
+            nc.sync.dma_start(
+                w4_plane[32 * q : 32 * q + 4, :].bitcast(I32), w4_scales[0, 4 * q : 4 * q + 4, :].bitcast(I32)
+            )
+        cache.append(load_page(page0, 3, "cache"))
+        idx4 = load_list(offs4, "idx4")
+        catalogue = [load_page(page1, u, "catalogue") for u in range(ROWT)]
+
+        w1_q.append([quantise_weight(w1_raw[1][a], "w1_1_%d" % a, "w1_bf", PASSES) for a in range(PASSES)])
+        put_state(1, 0, S)
+        first_stage(2)
+        put_state(2, 0, S)
+        first_stage(3)
+        w3_codes, w3_plane = quantise_weight(w3_raw, "w3", "w3_bf", 1)
+        put_state(3, 0, S)
+
+        die = keep.tile([P, ROWT, NP], F32, name="die", tag="state")
+        x_codes = keep.tile([P, NP], U32, name="x_codes", align_bytes=64)
+        x_plane = keep.tile([P, NP], U8, name="x_plane", align_bytes=64)
+        gate = keep.tile([P, 2, ROWT, HALF], F32, name="gate", tag="big", bufs=PASSES)
+        prod = keep.tile([P, 2, ROWT, HALF], F32, name="prod", tag="big", bufs=PASSES)
+
+        def recall(start, count):
+            for u in range(ROWT):
+                nc.vector.tensor_copy(
+                    die[:, u, start : start + count], cache[u][:].indirect(entries(idx3, start, count))
+                )
+
+        def make_x(c):
+            js = slice(CH * c, CH * (c + 1))
+            shifted = keep.tile([P, ROWT, CH], BF16, name="shifted", tag="shifted", bufs=4)
+            turned = psum.tile([P, CH // P, H], BF16, name="turned", tag="turn1", bufs=2)
+            for u in range(ROWT):
+                nc.scalar.activation(
+                    out=shifted[:, u, :], in_=die[:, u, js], func=ACT.Identity,
+                    bias=cols[:, ROWT + u : ROWT + u + 1],
+                )
+                for b in range(CH // P):
+                    nc.tensor.transpose(
+                        turned[:, b, P * u : P * (u + 1)], shifted[:, u, P * b : P * (b + 1)], ident_bf[:]
+                    )
+            pairs = keep.tile([P, CH // P, 2, P], F32, name="pairs", tag="pairs", bufs=2)
+            nc.scalar.copy(out=pairs[:], in_=turned[:].bitcast(F32).rearrange("j b (p w) -> j b w p", w=2))
+            back = psum.tile([P, CH // P, 2, P], F32, name="back", tag="turn2", bufs=2)
+            for b in range(CH // P):
+                for w in range(2):
+                    nc.tensor.transpose(back[:, b, w, :], pairs[:, b, w, :], ident[:])
+            grouped = keep.tile([P, CH // P, P, 2], F32, name="x_grouped", tag="x_grouped", bufs=4, align_bytes=64)
+            nc.scalar.copy(out=grouped[:], in_=back[:].rearrange("p b w j -> p b j w"))
+            nc.vector.quantize_mx(
+                out=x_codes[:, js].bitcast(FP8X4), scales=x_plane[:, js],
+                in_=grouped[:].rearrange("p b j w -> p (b j w)").bitcast(BF16),
+            )
+
+        def second_stage(hh, u):
+            js = slice(HALF * hh, HALF * (hh + 1))
+            ns = slice(P * u, P * (u + 1))
+            a_ps = psum.tile([P, HALF], F32, name="a_ps", tag="acc", bufs=4)
+            nc.tensor.matmul_mx(
+                out=a_ps[:], lhsT=w4_codes[:, 2 * P * u : 2 * P * (u + 1)].bitcast(FP4X4),
+                lhsT_scale=w4_plane[:, ns], rhs=x_codes[:, js].bitcast(FP8X4), rhs_scale=x_plane[:, js],
+                start=True, stop=True,
+            )
+            b_ps = psum.tile([P, HALF], F32, name="b_ps", tag="acc", bufs=4)
+            nc.tensor.matmul_mx(
+                out=b_ps[:], lhsT=w3_codes[:, ns].bitcast(FP8X4), lhsT_scale=w3_plane[:, ns],
+                rhs=x_codes[:, js].bitcast(FP8X4), rhs_scale=x_plane[:, js], start=True, stop=True,
+            )
+            nc.scalar.activation(out=gate[:, hh, u, :], in_=a_ps[:], func=ACT.Silu)
+            nc.vector.tensor_tensor(prod[:, hh, u, :], b_ps[:], die[:, u, js], MULT)
+            nc.vector.tensor_tensor(prod[:, hh, u, :], prod[:, hh, u, :], gate[:, hh, u, :], ADD)
+
+        def put_result(hh, u):
+            js = slice(HALF * hh, HALF * (hh + 1))
+            nc.vector.tensor_tensor(
+                catalogue[u][:].indirect(entries(idx4, HALF * hh, HALF)), prod[:, hh, u, :], wgo_sb[:, js], MULT
+            )
+
+        recall(0, CH)
+        make_x(0)
+        recall(CH, CH)
+        make_x(1)
+        recall(HALF, HALF)
+        for u in range(ROWT):
+            second_stage(0, u)
+        make_x(2)
+        make_x(3)
+        for u in range(ROWT):
+            put_result(0, u)
+        for u in range(ROWT):
+            second_stage(1, u)
+            put_result(1, u)
+            nc.sync.dma_start(out[P * u : P * (u + 1), :], catalogue[u][:])

@@ -16,14 +16,16 @@ FP8X4 = mybir.dt.float8_e4m3fn_x4
 FP4X4 = mybir.dt.float4_e2m1fn_x4
 ACT = mybir.ActivationFunctionType
 MULT = mybir.AluOpType.mult
-ADD = mybir.AluOpType.add
 
 P = 128
-PASSES = K // 512
-ROWT = H // P
+PACK = 4
+K_PASS = P * PACK
+PASSES = K // K_PASS
+QUADS = 4
+ROW_TILES = H // P
 HALF = 512
-CH = 256
-WCOL = 256
+QUARTER = 256
+PRODUCT_BANKS = 4
 
 
 def tile_list_coin_die_catalogue_kernel(
@@ -36,100 +38,124 @@ def tile_list_coin_die_catalogue_kernel(
         keep = ctx.enter_context(tc.tile_pool(name="keep", bufs=1))
         psum = ctx.enter_context(tc.psum_pool(name="psum", bufs=1))
 
-        def load_list(src, name):
-            tile = lists.tile([P, src.shape[1]], U16, name=name)
-            nc.sync.dma_start(tile[:], src)
-            return tile
-
-        def entries(tile, start, count):
-            return tile[:, start // 16 : (start + count) // 16]
-
-        scale_win = keep.tile([P, T], U8, name="scale_win")
-        nc.vector.memset(scale_win[:].bitcast(I32), 0)
+        scale_window = keep.tile([P, T], U8, name="scale_window")
+        nc.vector.memset(scale_window[:].bitcast(I32), 0)
         w4_plane = keep.tile([P, H], U8, name="w4_plane", align_bytes=64)
         nc.vector.memset(w4_plane[:].bitcast(I32), 0)
-        vec_rows = keep.tile([P, P], F32, name="vec_rows")
-        nc.gpsimd.memset(vec_rows[:], 0.0)
+        vector_rows = keep.tile([P, P], F32, name="vector_rows")
+        nc.vector.memset(vector_rows[:], 0.0)
         ident = keep.tile([P, P], F32, name="ident")
         make_identity(nc, ident[:])
         ident_bf = keep.tile([P, P], BF16, name="ident_bf")
         make_identity(nc, ident_bf[:])
+
+        warm = keep.tile([P, 1], F32, name="warm")
+        nc.scalar.activation(out=warm[:], in_=ident[:, 0:1], func=ACT.Silu)
+
+        def load_list(src, name):
+            tile = lists.tile([P, src.shape[1]], U16, name=name)
+            nc.sync.dma_start(tile[:], src)
+            return tile
 
         def load_words(a):
             tile = keep.tile([P, T], U32, name="words%d" % a, tag="big", bufs=PASSES)
             nc.sync.dma_start(tile[:].bitcast(I32), tab_words[a].rearrange("p t i -> p (t i)").bitcast(I32))
             return tile
 
-        def load_w1(g):
-            tiles = []
-            for a in range(PASSES):
-                raw = keep.tile([P, 4, WCOL], F32, name="w1_raw%d_%d" % (g, a), tag="w1_raw", bufs=PASSES)
-                rows = w1[512 * a : 512 * (a + 1), WCOL * g : WCOL * (g + 1)]
-                nc.sync.dma_start(raw[:], rows.rearrange("(p i) c -> p i c", i=4))
-                tiles.append(raw)
-            return tiles
+        def load_w1(a, c0, width, buffer=None):
+            if buffer is None:
+                buffer = keep.tile([P, PACK * width], F32, name="w1_raw%d_%d" % (c0, a))
+            raw = buffer[:, 0 : PACK * width].rearrange("p (i c) -> p i c", i=PACK)
+            rows = w1[K_PASS * a : K_PASS * (a + 1), c0 : c0 + width]
+            nc.sync.dma_start(raw, rows.rearrange("(p i) c -> p i c", i=PACK))
+            return raw
 
         def load_page(src, u, name):
             tile = keep.tile([P, T2], F32, name="%s_%d" % (name, u))
             nc.sync.dma_start(tile[:], src[P * u : P * (u + 1), :])
             return tile
 
-        def quantise_weight(raw, name, tag, bufs):
-            width = raw.shape[2]
-            grouped = keep.tile([P, width, 4], BF16, name=name + "_bf", tag=tag, bufs=bufs, align_bytes=64)
-            nc.scalar.copy(
-                out=grouped[:].rearrange("p (c n) i -> p c i n", n=4),
-                in_=raw[:].rearrange("p i (c n) -> p c i n", n=4),
-            )
-            codes = keep.tile([P, width], U32, name=name + "_codes", align_bytes=64)
-            plane = keep.tile([P, width], U8, name=name + "_plane", align_bytes=64)
-            nc.vector.quantize_mx(
-                out=codes[:].bitcast(FP8X4), scales=plane[:], in_=grouped[:].rearrange("p c i -> p (c i)")
-            )
-            return codes, plane
-
         words = [load_words(0)]
         idx = load_list(offs, "idx")
-        for q in range(4):
-            nc.scalar.dma_start(
-                scale_win[32 * q : 32 * q + 4 * PASSES, :].bitcast(I32),
-                tab_scales[:, 4 * q : 4 * q + 4, :].bitcast(I32),
+        for quad in range(QUADS):
+            nc.sync.dma_start(
+                scale_window[32 * quad : 32 * quad + 4 * PASSES, :].bitcast(I32),
+                tab_scales[:, 4 * quad : 4 * quad + 4, :].bitcast(I32),
             )
-        nc.scalar.dma_start(vec_rows[0:ROWT, :], gain.rearrange("(u p) -> u p", p=P))
-        nc.scalar.dma_start(vec_rows[ROWT : 2 * ROWT, :], wear.rearrange("(u p) -> u p", p=P))
         words.append(load_words(1))
-        w1_raw = [load_w1(0)]
+        nc.sync.dma_start(vector_rows[0:ROW_TILES, :], gain.rearrange("(u p) -> u p", p=P))
+        nc.sync.dma_start(vector_rows[ROW_TILES : 2 * ROW_TILES, :], wear.rearrange("(u p) -> u p", p=P))
+        w1_raw_first = [load_w1(a, 0, P) for a in range(PASSES)]
         words.append(load_words(2))
-        idx2 = load_list(offs2, "idx2")
         wgs_sb = keep.tile([P, S], F32, name="wgs_sb")
-        nc.sync.dma_start(wgs_sb[:], wgs)
+        nc.sync.dma_start(wgs_sb[:, 0:HALF], wgs[:, 0:HALF])
+        idx2 = load_list(offs2, "idx2")
         cache = [load_page(page0, 0, "cache")]
+        w1_raw_second = [load_w1(a, P, P) for a in range(PASSES)]
+        nc.sync.dma_start(wgs_sb[:, HALF:S], wgs[:, HALF:S])
+        cache.append(load_page(page0, 1, "cache"))
+        w1_last = keep.tile([P, HALF + S], F32, name="w1_raw_last")
+        w1_raw_rest = [load_w1(a, 2 * P, 2 * P, w1_last if a == PASSES - 1 else None) for a in range(PASSES)]
+        cache.append(load_page(page0, 2, "cache"))
+        w3_raw = keep.tile([P, PACK, H], F32, name="w3_raw", tag="w3", align_bytes=64)
+        nc.sync.dma_start(w3_raw[:], w3.rearrange("(p i) c -> p i c", i=PACK))
+        w4_codes = keep.tile([P, 2 * H], U8, name="w4_codes", align_bytes=64)
+        nc.sync.dma_start(w4_codes[:].bitcast(I32), w4_words[0].bitcast(I32))
+        for quad in range(QUADS):
+            nc.sync.dma_start(
+                w4_plane[32 * quad : 32 * quad + 4, :].bitcast(I32),
+                w4_scales[0, 4 * quad : 4 * quad + 4, :].bitcast(I32),
+            )
+        idx3 = load_list(offs3, "idx3")
+        wgo_sb = keep.tile([P, NP], F32, name="wgo_sb")
+        nc.sync.dma_start(wgo_sb[:], wgo)
+        idx4 = load_list(offs4, "idx4")
+        cache.append(load_page(page0, 3, "cache"))
+        catalogue = [load_page(page1, u, "catalogue") for u in range(ROW_TILES)]
 
-        vec_ps = psum.tile([P, P], F32, name="vec_ps", tag="turn2", bufs=2)
-        nc.tensor.transpose(vec_ps[:], vec_rows[:], ident[:])
-        cols = keep.tile([P, 2 * ROWT], F32, name="cols")
-        nc.scalar.copy(out=cols[:], in_=vec_ps[:, 0 : 2 * ROWT])
+        def entries(tile, start, count):
+            return tile[:, start // 16 : (start + count) // 16]
+
+        columns_ps = psum.tile([P, P], F32, name="columns_ps", tag="back")
+        nc.tensor.transpose(columns_ps[:], vector_rows[:], ident[:])
+        columns = keep.tile([P, 2 * ROW_TILES], F32, name="columns")
+        nc.scalar.activation(out=columns[:], in_=columns_ps[:, 0 : 2 * ROW_TILES], func=ACT.Copy)
+
+        def round_weight(raw, grouped):
+            nc.scalar.copy(
+                out=grouped.rearrange("p (c n i) -> p c i n", n=4, i=PACK),
+                in_=raw.rearrange("p i (c n) -> p c i n", n=4),
+            )
+
+        def quantise_w1(raws, name):
+            done = []
+            for a in range(PASSES):
+                width = raws[a].shape[2]
+                grouped = keep.tile([P, PACK * width], BF16, name=name + "_bf", tag="w1_bf", bufs=PASSES, align_bytes=64)
+                round_weight(raws[a], grouped[:])
+                codes = keep.tile([P, width], U32, name="%s%d_codes" % (name, a), align_bytes=64)
+                plane = keep.tile([P, width], U8, name="%s%d_plane" % (name, a), align_bytes=64)
+                nc.vector.quantize_mx(out=codes[:].bitcast(FP8X4), scales=plane[:], in_=grouped[:])
+                done.append((codes, plane))
+            return done
 
         v_words = [keep.tile([P, S], U32, name="v_words%d" % a, align_bytes=64) for a in range(PASSES)]
         v_plane = keep.tile([P, S], U8, name="v_plane", align_bytes=64)
         nc.vector.tensor_copy(v_words[0][:], words[0][:].indirect(idx[:]))
-        nc.vector.tensor_copy(v_plane[:], scale_win[:].indirect(idx[:]))
+        nc.vector.tensor_copy(v_plane[:], scale_window[:].indirect(idx[:]))
         nc.vector.tensor_copy(v_words[1][:], words[1][:].indirect(idx[:]))
-        w1_q = [[quantise_weight(w1_raw[0][a], "w1_0_%d" % a, "w1_bf", PASSES) for a in range(PASSES)]]
-        for hh in range(2):
-            nc.vector.tensor_copy(
-                v_words[2][:, HALF * hh : HALF * (hh + 1)], words[2][:].indirect(entries(idx, HALF * hh, HALF))
-            )
+        w1_first = quantise_w1(w1_raw_first, "w1_first")
+        for start in (0, HALF):
+            nc.vector.tensor_copy(v_words[2][:, start : start + HALF], words[2][:].indirect(entries(idx, start, HALF)))
 
-        h = keep.tile([P, ROWT, S], F32, name="h", tag="state")
+        tanh_h = keep.tile([P, ROW_TILES, S], F32, name="tanh_h", tag="state")
 
-        def first_stage(u):
-            g, m0 = divmod(P * u, WCOL)
-            for hh in range(2):
-                js = slice(HALF * hh, HALF * (hh + 1))
-                acc = psum.tile([P, HALF], F32, name="acc", tag="acc", bufs=4)
+        def first_stage(u, w1_passes, m0):
+            for start, bank in ((0, "turned"), (HALF, "y_ps")):
+                js = slice(start, start + HALF)
+                acc = psum.tile([P, HALF], F32, name="acc", tag=bank)
                 for a in range(PASSES):
-                    codes, plane = w1_q[g][a]
+                    codes, plane = w1_passes[a]
                     nc.tensor.matmul_mx(
                         out=acc[:],
                         lhsT=codes[:, m0 : m0 + P].bitcast(FP8X4),
@@ -139,120 +165,157 @@ def tile_list_coin_die_catalogue_kernel(
                         start=(a == 0),
                         stop=(a == PASSES - 1),
                     )
-                nc.scalar.activation(out=h[:, u, js], in_=acc[:], func=ACT.Tanh)
-                nc.scalar.activation(out=h[:, u, js], in_=h[:, u, js], func=ACT.Copy, scale=cols[:, u : u + 1])
+                nc.scalar.activation(out=tanh_h[:, u, js], in_=acc[:], func=ACT.Tanh)
+
+        early_factor = keep.tile([P, 2, S], F32, name="early_factor", tag="big", bufs=PASSES)
+
+        def factor(u, start, count):
+            if u == 1 and start == HALF:
+                return w1_last[:, 0:count]
+            if u == 2:
+                return w1_last[:, HALF + start : HALF + start + count]
+            if u == 3:
+                return w3_raw[:].rearrange("p i c -> p (i c)")[:, start : start + count]
+            return early_factor[:, u, start : start + count]
+
+        def make_factor(u, start, count):
+            nc.scalar.activation(
+                out=factor(u, start, count), in_=wgs_sb[:, start : start + count], func=ACT.Copy, scale=columns[:, u : u + 1]
+            )
 
         def put_state(u, start, count):
-            js = slice(start, start + count)
             nc.vector.tensor_tensor(
-                cache[u][:].indirect(entries(idx2, start, count)), h[:, u, js], wgs_sb[:, js], MULT
+                cache[u][:].indirect(entries(idx2, start, count)), tanh_h[:, u, start : start + count],
+                factor(u, start, count), MULT,
             )
 
-        first_stage(0)
+        make_factor(0, 0, HALF)
+        first_stage(0, w1_first, 0)
         put_state(0, 0, HALF)
+        w1_second = quantise_w1(w1_raw_second, "w1_second")
+        make_factor(0, HALF, HALF)
         put_state(0, HALF, HALF)
-        first_stage(1)
-
-        w1_raw.append(load_w1(1))
-        wgo_sb = keep.tile([P, NP], F32, name="wgo_sb")
-        nc.sync.dma_start(wgo_sb[:], wgo)
-        cache.append(load_page(page0, 1, "cache"))
-        cache.append(load_page(page0, 2, "cache"))
-        w3_raw = keep.tile([P, 4, H], F32, name="w3_raw")
-        nc.sync.dma_start(w3_raw[:], w3.rearrange("(p i) c -> p i c", i=4))
-        idx3 = load_list(offs3, "idx3")
-        w4_codes = keep.tile([P, 2 * H], U8, name="w4_codes", align_bytes=64)
-        nc.sync.dma_start(w4_codes[:].bitcast(I32), w4_words[0].bitcast(I32))
-        for q in range(4):
-            nc.sync.dma_start(
-                w4_plane[32 * q : 32 * q + 4, :].bitcast(I32), w4_scales[0, 4 * q : 4 * q + 4, :].bitcast(I32)
-            )
-        cache.append(load_page(page0, 3, "cache"))
-        idx4 = load_list(offs4, "idx4")
-        catalogue = [load_page(page1, u, "catalogue") for u in range(ROWT)]
-
-        w1_q.append([quantise_weight(w1_raw[1][a], "w1_1_%d" % a, "w1_bf", PASSES) for a in range(PASSES)])
-        put_state(1, 0, S)
-        first_stage(2)
+        make_factor(1, 0, HALF)
+        first_stage(1, w1_second, 0)
+        put_state(1, 0, HALF)
+        w1_rest = quantise_w1(w1_raw_rest, "w1_rest")
+        make_factor(1, HALF, HALF)
+        put_state(1, HALF, HALF)
+        make_factor(2, 0, S)
+        first_stage(2, w1_rest, 0)
+        first_stage(3, w1_rest, P)
+        w3_bf = keep.tile([P, PACK * H], BF16, name="w3_bf", align_bytes=64)
+        round_weight(w3_raw[:], w3_bf[:])
         put_state(2, 0, S)
-        first_stage(3)
-        w3_codes, w3_plane = quantise_weight(w3_raw, "w3", "w3_bf", 1)
+        make_factor(3, 0, S)
         put_state(3, 0, S)
 
-        die = keep.tile([P, ROWT, NP], F32, name="die", tag="state")
+        recalled = keep.tile([P, ROW_TILES * NP], F32, name="recalled", tag="state")
+        w3_codes = keep.tile([P, H], U32, name="w3_codes", tag="w3", align_bytes=64)
+        w3_plane = keep.tile([P, H], U8, name="w3_plane", align_bytes=64)
+        x_grouped = [keep.tile([P, HALF], F32, name="x_grouped%d" % c, align_bytes=64) for c in range(NP // QUARTER)]
+        stage = [keep.tile([P, HALF], F32, name="stage%d" % n) for n in range(2)]
         x_codes = keep.tile([P, NP], U32, name="x_codes", align_bytes=64)
         x_plane = keep.tile([P, NP], U8, name="x_plane", align_bytes=64)
-        gate = keep.tile([P, 2, ROWT, HALF], F32, name="gate", tag="big", bufs=PASSES)
-        prod = keep.tile([P, 2, ROWT, HALF], F32, name="prod", tag="big", bufs=PASSES)
+        gate = keep.tile([P, ROW_TILES, NP], F32, name="gate", tag="big", bufs=PASSES)
+        prod = keep.tile([P, ROW_TILES, NP], F32, name="prod", tag="big", bufs=PASSES)
 
-        def recall(start, count):
-            for u in range(ROWT):
-                nc.vector.tensor_copy(
-                    die[:, u, start : start + count], cache[u][:].indirect(entries(idx3, start, count))
-                )
+        def die(u, start, count):
+            if u >= 2 and start >= HALF:
+                return x_grouped[u - 2][:, start - HALF : start - HALF + count]
+            return recalled[:, NP * u + start : NP * u + start + count]
 
-        def make_x(c):
-            js = slice(CH * c, CH * (c + 1))
-            shifted = keep.tile([P, ROWT, CH], BF16, name="shifted", tag="shifted", bufs=4)
-            turned = psum.tile([P, CH // P, H], BF16, name="turned", tag="turn1", bufs=2)
-            for u in range(ROWT):
-                nc.scalar.activation(
-                    out=shifted[:, u, :], in_=die[:, u, js], func=ACT.Identity,
-                    bias=cols[:, ROWT + u : ROWT + u + 1],
-                )
-                for b in range(CH // P):
-                    nc.tensor.transpose(
-                        turned[:, b, P * u : P * (u + 1)], shifted[:, u, P * b : P * (b + 1)], ident_bf[:]
-                    )
-            pairs = keep.tile([P, CH // P, 2, P], F32, name="pairs", tag="pairs", bufs=2)
-            nc.scalar.copy(out=pairs[:], in_=turned[:].bitcast(F32).rearrange("j b (p w) -> j b w p", w=2))
-            back = psum.tile([P, CH // P, 2, P], F32, name="back", tag="turn2", bufs=2)
-            for b in range(CH // P):
-                for w in range(2):
-                    nc.tensor.transpose(back[:, b, w, :], pairs[:, b, w, :], ident[:])
-            grouped = keep.tile([P, CH // P, P, 2], F32, name="x_grouped", tag="x_grouped", bufs=4, align_bytes=64)
-            nc.scalar.copy(out=grouped[:], in_=back[:].rearrange("p b w j -> p b j w"))
-            nc.vector.quantize_mx(
-                out=x_codes[:, js].bitcast(FP8X4), scales=x_plane[:, js],
-                in_=grouped[:].rearrange("p b j w -> p (b j w)").bitcast(BF16),
+        def recall(u, start, count):
+            nc.vector.tensor_copy(die(u, start, count), cache[u][:].indirect(entries(idx3, start, count)))
+
+        def shift(u, c, buffer):
+            shifted = buffer.bitcast(BF16).rearrange("p (u j) -> p u j", u=ROW_TILES)
+            nc.scalar.activation(
+                out=shifted[:, u, :], in_=die(u, QUARTER * c, QUARTER), func=ACT.Identity,
+                bias=columns[:, ROW_TILES + u : ROW_TILES + u + 1],
             )
 
-        def second_stage(hh, u):
-            js = slice(HALF * hh, HALF * (hh + 1))
+        def quantise_x(c, buffer, pairs, turn_bank):
+            shifted = buffer.bitcast(BF16).rearrange("p (u j) -> p u j", u=ROW_TILES)
+            blocks = QUARTER // P
+            turned = psum.tile([P, blocks, H], BF16, name="turned", tag=turn_bank)
+            for u in range(ROW_TILES):
+                for b in range(blocks):
+                    nc.tensor.transpose(turned[:, b, P * u : P * (u + 1)], shifted[:, u, P * b : P * (b + 1)], ident_bf[:])
+            by_pair = pairs.rearrange("j (b w p) -> j b w p", w=2, p=P)
+            nc.scalar.copy(out=by_pair, in_=turned[:].bitcast(F32).rearrange("j b (p w) -> j b w p", w=2))
+            back = psum.tile([P, blocks, 2, P], F32, name="back", tag="back")
+            for b in range(blocks):
+                for w in range(2):
+                    nc.tensor.transpose(back[:, b, w, :], by_pair[:, b, w, :], ident[:])
+            nc.scalar.copy(
+                out=x_grouped[c][:].rearrange("p (b j w) -> p b j w", j=P, w=2),
+                in_=back[:].rearrange("p b w j -> p b j w"),
+            )
+            js = slice(QUARTER * c, QUARTER * (c + 1))
+            nc.vector.quantize_mx(
+                out=x_codes[:, js].bitcast(FP8X4), scales=x_plane[:, js], in_=x_grouped[c][:].bitcast(BF16)
+            )
+
+        def second_stage(u, start, count):
+            js = slice(start, start + count)
             ns = slice(P * u, P * (u + 1))
-            a_ps = psum.tile([P, HALF], F32, name="a_ps", tag="acc", bufs=4)
+            b_ps = psum.tile([P, count], F32, name="b_ps", tag="product", bufs=PRODUCT_BANKS)
+            nc.tensor.matmul_mx(
+                out=b_ps[:], lhsT=w3_codes[:, ns].bitcast(FP8X4), lhsT_scale=w3_plane[:, ns],
+                rhs=x_codes[:, js].bitcast(FP8X4), rhs_scale=x_plane[:, js], start=True, stop=True,
+            )
+            a_ps = psum.tile([P, count], F32, name="a_ps", tag="product", bufs=PRODUCT_BANKS)
             nc.tensor.matmul_mx(
                 out=a_ps[:], lhsT=w4_codes[:, 2 * P * u : 2 * P * (u + 1)].bitcast(FP4X4),
                 lhsT_scale=w4_plane[:, ns], rhs=x_codes[:, js].bitcast(FP8X4), rhs_scale=x_plane[:, js],
                 start=True, stop=True,
             )
-            b_ps = psum.tile([P, HALF], F32, name="b_ps", tag="acc", bufs=4)
-            nc.tensor.matmul_mx(
-                out=b_ps[:], lhsT=w3_codes[:, ns].bitcast(FP8X4), lhsT_scale=w3_plane[:, ns],
-                rhs=x_codes[:, js].bitcast(FP8X4), rhs_scale=x_plane[:, js], start=True, stop=True,
-            )
-            nc.scalar.activation(out=gate[:, hh, u, :], in_=a_ps[:], func=ACT.Silu)
-            nc.vector.tensor_tensor(prod[:, hh, u, :], b_ps[:], die[:, u, js], MULT)
-            nc.vector.tensor_tensor(prod[:, hh, u, :], prod[:, hh, u, :], gate[:, hh, u, :], ADD)
+            nc.scalar.activation(out=gate[:, u, js], in_=a_ps[:], func=ACT.Silu)
+            nc.vector.tensor_tensor(prod[:, u, js], b_ps[:], die(u, start, count), MULT)
+            summed = psum.tile([P, count], F32, name="summed", tag="summed")
+            for b0 in range(0, count, P):
+                bs = slice(start + b0, start + b0 + P)
+                nc.tensor.matmul(summed[:, b0 : b0 + P], prod[:, u, bs], ident[:], start=True, stop=False, is_transpose=True)
+                nc.tensor.matmul(summed[:, b0 : b0 + P], gate[:, u, bs], ident[:], start=False, stop=True, is_transpose=True)
+            nc.scalar.copy(out=gate[:, u, js], in_=summed[:])
 
-        def put_result(hh, u):
-            js = slice(HALF * hh, HALF * (hh + 1))
+        def put_result(u, start, count):
+            js = slice(start, start + count)
+            y_ps = psum.tile([P, count], F32, name="y_ps", tag="y_ps")
+            for b0 in range(0, count, P):
+                nc.tensor.transpose(y_ps[:, b0 : b0 + P], gate[:, u, start + b0 : start + b0 + P], ident[:])
+            nc.scalar.copy(out=prod[:, u, js], in_=y_ps[:])
             nc.vector.tensor_tensor(
-                catalogue[u][:].indirect(entries(idx4, HALF * hh, HALF)), prod[:, hh, u, :], wgo_sb[:, js], MULT
+                catalogue[u][:].indirect(entries(idx4, start, count)), prod[:, u, js], wgo_sb[:, js], MULT
             )
 
-        recall(0, CH)
-        make_x(0)
-        recall(CH, CH)
-        make_x(1)
-        recall(HALF, HALF)
-        for u in range(ROWT):
-            second_stage(0, u)
-        make_x(2)
-        make_x(3)
-        for u in range(ROWT):
-            put_result(0, u)
-        for u in range(ROWT):
-            second_stage(1, u)
-            put_result(1, u)
+        for c, turn_bank in ((0, "turned"), (1, "summed")):
+            buffer = keep.tile([P, HALF], F32, name="shifted%d" % c)[:]
+            for u in range(ROW_TILES):
+                recall(u, QUARTER * c, QUARTER)
+                shift(u, c, buffer)
+            quantise_x(c, buffer, stage[c][:], turn_bank)
+        nc.vector.quantize_mx(out=w3_codes[:].bitcast(FP8X4), scales=w3_plane[:], in_=w3_bf[:])
+        for u in range(ROW_TILES - 1):
+            recall(u, HALF, HALF)
+
+        for u in range(ROW_TILES):
+            second_stage(u, 0, QUARTER)
+        recall(ROW_TILES - 1, HALF, HALF)
+        for u in range(ROW_TILES):
+            put_result(u, 0, QUARTER)
+        for u in range(ROW_TILES):
+            second_stage(u, QUARTER, QUARTER)
+        for c in range(2, 4):
+            for u in range(ROW_TILES):
+                shift(u, c, stage[(c + 1) % 2][:])
+            quantise_x(c, stage[(c + 1) % 2][:], stage[c % 2][:], "turned")
+        for u in range(ROW_TILES):
+            put_result(u, QUARTER, QUARTER)
+
+        for u in range(ROW_TILES):
+            second_stage(u, HALF, HALF)
+        for u in range(ROW_TILES):
+            put_result(u, HALF, HALF)
             nc.sync.dma_start(out[P * u : P * (u + 1), :], catalogue[u][:])

@@ -16,6 +16,7 @@ FP8X4 = mybir.dt.float8_e4m3fn_x4
 FP4X4 = mybir.dt.float4_e2m1fn_x4
 ACT = mybir.ActivationFunctionType
 MULT = mybir.AluOpType.mult
+ADD = mybir.AluOpType.add
 
 P = 128
 PACK = 4
@@ -42,15 +43,12 @@ def tile_list_coin_die_catalogue_kernel(
         nc.vector.memset(scale_window[:].bitcast(I32), 0)
         w4_plane = keep.tile([P, H], U8, name="w4_plane", align_bytes=64)
         nc.vector.memset(w4_plane[:].bitcast(I32), 0)
-        vector_rows = keep.tile([P, P], F32, name="vector_rows")
-        nc.vector.memset(vector_rows[:], 0.0)
         ident = keep.tile([P, P], F32, name="ident")
         make_identity(nc, ident[:])
         ident_bf = keep.tile([P, P], BF16, name="ident_bf")
         make_identity(nc, ident_bf[:])
-
-        warm = keep.tile([P, 1], F32, name="warm")
-        nc.scalar.activation(out=warm[:], in_=ident[:, 0:1], func=ACT.Silu)
+        vector_rows = keep.tile([P, P], F32, name="vector_rows")
+        nc.scalar.activation(out=vector_rows[:], in_=ident[:], func=ACT.Silu, scale=0.0)
 
         def load_list(src, name):
             tile = lists.tile([P, src.shape[1]], U16, name=name)
@@ -257,6 +255,9 @@ def tile_list_coin_die_catalogue_kernel(
                 out=x_codes[:, js].bitcast(FP8X4), scales=x_plane[:, js], in_=x_grouped[c][:].bitcast(BF16)
             )
 
+        def added_on_vector(u, start):
+            return u == 0 and start > 0
+
         def second_stage(u, start, count):
             js = slice(start, start + count)
             ns = slice(P * u, P * (u + 1))
@@ -273,6 +274,9 @@ def tile_list_coin_die_catalogue_kernel(
             )
             nc.scalar.activation(out=gate[:, u, js], in_=a_ps[:], func=ACT.Silu)
             nc.vector.tensor_tensor(prod[:, u, js], b_ps[:], die(u, start, count), MULT)
+            if added_on_vector(u, start):
+                nc.vector.tensor_tensor(prod[:, u, js], prod[:, u, js], gate[:, u, js], ADD)
+                return
             summed = psum.tile([P, count], F32, name="summed", tag="summed")
             for b0 in range(0, count, P):
                 bs = slice(start + b0, start + b0 + P)
@@ -282,10 +286,11 @@ def tile_list_coin_die_catalogue_kernel(
 
         def put_result(u, start, count):
             js = slice(start, start + count)
-            y_ps = psum.tile([P, count], F32, name="y_ps", tag="y_ps")
-            for b0 in range(0, count, P):
-                nc.tensor.transpose(y_ps[:, b0 : b0 + P], gate[:, u, start + b0 : start + b0 + P], ident[:])
-            nc.scalar.copy(out=prod[:, u, js], in_=y_ps[:])
+            if not added_on_vector(u, start):
+                y_ps = psum.tile([P, count], F32, name="y_ps", tag="y_ps")
+                for b0 in range(0, count, P):
+                    nc.tensor.transpose(y_ps[:, b0 : b0 + P], gate[:, u, start + b0 : start + b0 + P], ident[:])
+                nc.scalar.copy(out=prod[:, u, js], in_=y_ps[:])
             nc.vector.tensor_tensor(
                 catalogue[u][:].indirect(entries(idx4, start, count)), prod[:, u, js], wgo_sb[:, js], MULT
             )

@@ -56,7 +56,10 @@ def tile_list_coin_die_catalogue_kernel(
             return tile
 
         def load_words(a):
-            tile = keep.tile([P, T], U32, name="words%d" % a, tag="big", bufs=PASSES)
+            if a == 1:
+                tile = keep.tile([P, T], U32, name="words1", tag="words1", align_bytes=64)
+            else:
+                tile = keep.tile([P, T], U32, name="words%d" % a, tag="big", bufs=2)
             nc.sync.dma_start(tile[:].bitcast(I32), tab_words[a].rearrange("p t i -> p (t i)").bitcast(I32))
             return tile
 
@@ -76,7 +79,7 @@ def tile_list_coin_die_catalogue_kernel(
         words = [load_words(0)]
         idx = load_list(offs, "idx")
         for quad in range(QUADS):
-            nc.sync.dma_start(
+            nc.gpsimd.dma_start(
                 scale_window[32 * quad : 32 * quad + 4 * PASSES, :].bitcast(I32),
                 tab_scales[:, 4 * quad : 4 * quad + 4, :].bitcast(I32),
             )
@@ -138,10 +141,10 @@ def tile_list_coin_die_catalogue_kernel(
             return done
 
         v_words = [keep.tile([P, S], U32, name="v_words%d" % a, align_bytes=64) for a in range(PASSES)]
-        v_plane = keep.tile([P, S], U8, name="v_plane", align_bytes=64)
+        v_plane = keep.tile([P, S], U8, name="v_plane", tag="words1", align_bytes=64)
         nc.vector.tensor_copy(v_words[0][:], words[0][:].indirect(idx[:]))
-        nc.vector.tensor_copy(v_plane[:], scale_window[:].indirect(idx[:]))
         nc.vector.tensor_copy(v_words[1][:], words[1][:].indirect(idx[:]))
+        nc.vector.tensor_copy(v_plane[:], scale_window[:].indirect(idx[:]))
         w1_first = quantise_w1(w1_raw_first, "w1_first")
         for start in (0, HALF):
             nc.vector.tensor_copy(v_words[2][:, start : start + HALF], words[2][:].indirect(entries(idx, start, HALF)))
@@ -165,7 +168,7 @@ def tile_list_coin_die_catalogue_kernel(
                     )
                 nc.scalar.activation(out=tanh_h[:, u, js], in_=acc[:], func=ACT.Tanh)
 
-        early_factor = keep.tile([P, 2, S], F32, name="early_factor", tag="big", bufs=PASSES)
+        early_factor = keep.tile([P, 2, S], F32, name="early_factor", tag="big", bufs=2)
 
         def factor(u, start, count):
             if u == 1 and start == HALF:
@@ -215,8 +218,8 @@ def tile_list_coin_die_catalogue_kernel(
         stage = [keep.tile([P, HALF], F32, name="stage%d" % n) for n in range(2)]
         x_codes = keep.tile([P, NP], U32, name="x_codes", align_bytes=64)
         x_plane = keep.tile([P, NP], U8, name="x_plane", align_bytes=64)
-        gate = keep.tile([P, ROW_TILES, NP], F32, name="gate", tag="big", bufs=PASSES)
-        prod = keep.tile([P, ROW_TILES, NP], F32, name="prod", tag="big", bufs=PASSES)
+        gate = keep.tile([P, ROW_TILES, NP], F32, name="gate", tag="big", bufs=2)
+        prod = keep.tile([P, ROW_TILES, NP], F32, name="prod", tag="big", bufs=2)
 
         def die(u, start, count):
             if u >= 2 and start >= HALF:

from contextlib import ExitStack

import concourse.mybir as mybir
from concourse.masks import make_identity

K, T, S, H, T2, NP = 1536, 4096, 1024, 512, 2048, 1024
FLOPS = 2 * K * H * S + 2 * 2 * H * H * NP

F32 = mybir.dt.float32
BF16 = mybir.dt.bfloat16
I32 = mybir.dt.int32
U32 = mybir.dt.uint32
U16 = mybir.dt.uint16
U8 = mybir.dt.uint8
FP8X4 = mybir.dt.float8_e4m3fn_x4
FP4X4 = mybir.dt.float4_e2m1fn_x4
ACT = mybir.ActivationFunctionType
MULT = mybir.AluOpType.mult
ADD = mybir.AluOpType.add

P = 128
PACK = 4
K_PASS = P * PACK
PASSES = K // K_PASS
QUADS = 4
ROW_TILES = H // P
HALF = 512
QUARTER = 256
PRODUCT_BANKS = 4


def tile_list_coin_die_catalogue_kernel(
    tc, tab_words, tab_scales, offs, offs2, offs3, offs4, w1, gain, wgs, page0, wear,
    w4_words, w4_scales, w3, wgo, page1, out,
):
    nc = tc.nc
    with ExitStack() as ctx:
        lists = ctx.enter_context(tc.tile_pool(name="lists", bufs=1))
        keep = ctx.enter_context(tc.tile_pool(name="keep", bufs=1))
        psum = ctx.enter_context(tc.psum_pool(name="psum", bufs=1))

        scale_window = keep.tile([P, T], U8, name="scale_window")
        nc.vector.memset(scale_window[:].bitcast(I32), 0)
        w4_plane = keep.tile([P, H], U8, name="w4_plane", align_bytes=64)
        nc.vector.memset(w4_plane[:].bitcast(I32), 0)
        ident = keep.tile([P, P], F32, name="ident")
        make_identity(nc, ident[:])
        ident_bf = keep.tile([P, P], BF16, name="ident_bf")
        make_identity(nc, ident_bf[:])
        vector_rows = keep.tile([P, P], F32, name="vector_rows")
        nc.scalar.activation(out=vector_rows[:], in_=ident[:], func=ACT.Silu, scale=0.0)

        def load_list(src, name):
            tile = lists.tile([P, src.shape[1]], U16, name=name)
            nc.sync.dma_start(tile[:], src)
            return tile

        def load_words(a):
            if a == 1:
                tile = keep.tile([P, T], U32, name="words1", tag="words1", align_bytes=64)
            else:
                tile = keep.tile([P, T], U32, name="words%d" % a, tag="big", bufs=2)
            nc.sync.dma_start(tile[:].bitcast(I32), tab_words[a].rearrange("p t i -> p (t i)").bitcast(I32))
            return tile

        def load_w1(a, c0, width, buffer=None):
            if buffer is None:
                buffer = keep.tile([P, PACK * width], F32, name="w1_raw%d_%d" % (c0, a))
            raw = buffer[:, 0 : PACK * width].rearrange("p (i c) -> p i c", i=PACK)
            rows = w1[K_PASS * a : K_PASS * (a + 1), c0 : c0 + width]
            nc.sync.dma_start(raw, rows.rearrange("(p i) c -> p i c", i=PACK))
            return raw

        def load_page(src, u, name):
            tile = keep.tile([P, T2], F32, name="%s_%d" % (name, u))
            nc.sync.dma_start(tile[:], src[P * u : P * (u + 1), :])
            return tile

        words = [load_words(0)]
        idx = load_list(offs, "idx")
        for quad in range(QUADS):
            nc.gpsimd.dma_start(
                scale_window[32 * quad : 32 * quad + 4 * PASSES, :].bitcast(I32),
                tab_scales[:, 4 * quad : 4 * quad + 4, :].bitcast(I32),
            )
        words.append(load_words(1))
        nc.sync.dma_start(vector_rows[0:ROW_TILES, :], gain.rearrange("(u p) -> u p", p=P))
        nc.sync.dma_start(vector_rows[ROW_TILES : 2 * ROW_TILES, :], wear.rearrange("(u p) -> u p", p=P))
        w1_raw_first = [load_w1(a, 0, P) for a in range(PASSES)]
        words.append(load_words(2))
        wgs_sb = keep.tile([P, S], F32, name="wgs_sb")
        nc.sync.dma_start(wgs_sb[:, 0:HALF], wgs[:, 0:HALF])
        idx2 = load_list(offs2, "idx2")
        cache = [load_page(page0, 0, "cache")]
        w1_raw_second = [load_w1(a, P, P) for a in range(PASSES)]
        nc.sync.dma_start(wgs_sb[:, HALF:S], wgs[:, HALF:S])
        cache.append(load_page(page0, 1, "cache"))
        w1_last = keep.tile([P, HALF + S], F32, name="w1_raw_last")
        w1_raw_rest = [load_w1(a, 2 * P, 2 * P, w1_last if a == PASSES - 1 else None) for a in range(PASSES)]
        cache.append(load_page(page0, 2, "cache"))
        w3_raw = keep.tile([P, PACK, H], F32, name="w3_raw", tag="w3", align_bytes=64)
        nc.sync.dma_start(w3_raw[:], w3.rearrange("(p i) c -> p i c", i=PACK))
        w4_codes = keep.tile([P, 2 * H], U8, name="w4_codes", align_bytes=64)
        nc.sync.dma_start(w4_codes[:].bitcast(I32), w4_words[0].bitcast(I32))
        for quad in range(QUADS):
            nc.sync.dma_start(
                w4_plane[32 * quad : 32 * quad + 4, :].bitcast(I32),
                w4_scales[0, 4 * quad : 4 * quad + 4, :].bitcast(I32),
            )
        idx3 = load_list(offs3, "idx3")
        wgo_sb = keep.tile([P, NP], F32, name="wgo_sb")
        nc.sync.dma_start(wgo_sb[:], wgo)
        idx4 = load_list(offs4, "idx4")
        cache.append(load_page(page0, 3, "cache"))
        catalogue = [load_page(page1, u, "catalogue") for u in range(ROW_TILES)]

        def entries(tile, start, count):
            return tile[:, start // 16 : (start + count) // 16]

        columns_ps = psum.tile([P, P], F32, name="columns_ps", tag="back")
        nc.tensor.transpose(columns_ps[:], vector_rows[:], ident[:])
        columns = keep.tile([P, 2 * ROW_TILES], F32, name="columns")
        nc.scalar.activation(out=columns[:], in_=columns_ps[:, 0 : 2 * ROW_TILES], func=ACT.Copy)

        def round_weight(raw, grouped):
            nc.scalar.copy(
                out=grouped.rearrange("p (c n i) -> p c i n", n=4, i=PACK),
                in_=raw.rearrange("p i (c n) -> p c i n", n=4),
            )

        def quantise_w1(raws, name):
            done = []
            for a in range(PASSES):
                width = raws[a].shape[2]
                grouped = keep.tile([P, PACK * width], BF16, name=name + "_bf", tag="w1_bf", bufs=PASSES, align_bytes=64)
                round_weight(raws[a], grouped[:])
                codes = keep.tile([P, width], U32, name="%s%d_codes" % (name, a), align_bytes=64)
                plane = keep.tile([P, width], U8, name="%s%d_plane" % (name, a), align_bytes=64)
                nc.vector.quantize_mx(out=codes[:].bitcast(FP8X4), scales=plane[:], in_=grouped[:])
                done.append((codes, plane))
            return done

        v_words = [keep.tile([P, S], U32, name="v_words%d" % a, align_bytes=64) for a in range(PASSES)]
        v_plane = keep.tile([P, S], U8, name="v_plane", tag="words1", align_bytes=64)
        nc.vector.tensor_copy(v_words[0][:], words[0][:].indirect(idx[:]))
        nc.vector.tensor_copy(v_words[1][:], words[1][:].indirect(idx[:]))
        nc.vector.tensor_copy(v_plane[:], scale_window[:].indirect(idx[:]))
        w1_first = quantise_w1(w1_raw_first, "w1_first")
        for start in (0, HALF):
            nc.vector.tensor_copy(v_words[2][:, start : start + HALF], words[2][:].indirect(entries(idx, start, HALF)))

        tanh_h = keep.tile([P, ROW_TILES, S], F32, name="tanh_h", tag="state")

        def first_stage(u, w1_passes, m0):
            for start, bank in ((0, "turned"), (HALF, "y_ps")):
                js = slice(start, start + HALF)
                acc = psum.tile([P, HALF], F32, name="acc", tag=bank)
                for a in range(PASSES):
                    codes, plane = w1_passes[a]
                    nc.tensor.matmul_mx(
                        out=acc[:],
                        lhsT=codes[:, m0 : m0 + P].bitcast(FP8X4),
                        lhsT_scale=plane[:, m0 : m0 + P],
                        rhs=v_words[a][:, js].bitcast(FP8X4),
                        rhs_scale=v_plane[4 * a : P, js],
                        start=(a == 0),
                        stop=(a == PASSES - 1),
                    )
                nc.scalar.activation(out=tanh_h[:, u, js], in_=acc[:], func=ACT.Tanh)

        early_factor = keep.tile([P, 2, S], F32, name="early_factor", tag="big", bufs=2)

        def factor(u, start, count):
            if u == 1 and start == HALF:
                return w1_last[:, 0:count]
            if u == 2:
                return w1_last[:, HALF + start : HALF + start + count]
            if u == 3:
                return w3_raw[:].rearrange("p i c -> p (i c)")[:, start : start + count]
            return early_factor[:, u, start : start + count]

        def make_factor(u, start, count):
            nc.scalar.activation(
                out=factor(u, start, count), in_=wgs_sb[:, start : start + count], func=ACT.Copy, scale=columns[:, u : u + 1]
            )

        def put_state(u, start, count):
            nc.vector.tensor_tensor(
                cache[u][:].indirect(entries(idx2, start, count)), tanh_h[:, u, start : start + count],
                factor(u, start, count), MULT,
            )

        make_factor(0, 0, HALF)
        first_stage(0, w1_first, 0)
        put_state(0, 0, HALF)
        w1_second = quantise_w1(w1_raw_second, "w1_second")
        make_factor(0, HALF, HALF)
        put_state(0, HALF, HALF)
        make_factor(1, 0, HALF)
        first_stage(1, w1_second, 0)
        put_state(1, 0, HALF)
        w1_rest = quantise_w1(w1_raw_rest, "w1_rest")
        make_factor(1, HALF, HALF)
        put_state(1, HALF, HALF)
        make_factor(2, 0, S)
        first_stage(2, w1_rest, 0)
        first_stage(3, w1_rest, P)
        w3_bf = keep.tile([P, PACK * H], BF16, name="w3_bf", align_bytes=64)
        round_weight(w3_raw[:], w3_bf[:])
        put_state(2, 0, S)
        make_factor(3, 0, S)
        put_state(3, 0, S)

        recalled = keep.tile([P, ROW_TILES * NP], F32, name="recalled", tag="state")
        w3_codes = keep.tile([P, H], U32, name="w3_codes", tag="w3", align_bytes=64)
        w3_plane = keep.tile([P, H], U8, name="w3_plane", align_bytes=64)
        x_grouped = [keep.tile([P, HALF], F32, name="x_grouped%d" % c, align_bytes=64) for c in range(NP // QUARTER)]
        stage = [keep.tile([P, HALF], F32, name="stage%d" % n) for n in range(2)]
        x_codes = keep.tile([P, NP], U32, name="x_codes", align_bytes=64)
        x_plane = keep.tile([P, NP], U8, name="x_plane", align_bytes=64)
        gate = keep.tile([P, ROW_TILES, NP], F32, name="gate", tag="big", bufs=2)
        prod = keep.tile([P, ROW_TILES, NP], F32, name="prod", tag="big", bufs=2)

        def die(u, start, count):
            if u >= 2 and start >= HALF:
                return x_grouped[u - 2][:, start - HALF : start - HALF + count]
            return recalled[:, NP * u + start : NP * u + start + count]

        def recall(u, start, count):
            nc.vector.tensor_copy(die(u, start, count), cache[u][:].indirect(entries(idx3, start, count)))

        def shift(u, c, buffer):
            shifted = buffer.bitcast(BF16).rearrange("p (u j) -> p u j", u=ROW_TILES)
            nc.scalar.activation(
                out=shifted[:, u, :], in_=die(u, QUARTER * c, QUARTER), func=ACT.Identity,
                bias=columns[:, ROW_TILES + u : ROW_TILES + u + 1],
            )

        def quantise_x(c, buffer, pairs, turn_bank):
            shifted = buffer.bitcast(BF16).rearrange("p (u j) -> p u j", u=ROW_TILES)
            blocks = QUARTER // P
            turned = psum.tile([P, blocks, H], BF16, name="turned", tag=turn_bank)
            for u in range(ROW_TILES):
                for b in range(blocks):
                    nc.tensor.transpose(turned[:, b, P * u : P * (u + 1)], shifted[:, u, P * b : P * (b + 1)], ident_bf[:])
            by_pair = pairs.rearrange("j (b w p) -> j b w p", w=2, p=P)
            nc.scalar.copy(out=by_pair, in_=turned[:].bitcast(F32).rearrange("j b (p w) -> j b w p", w=2))
            back = psum.tile([P, blocks, 2, P], F32, name="back", tag="back")
            for b in range(blocks):
                for w in range(2):
                    nc.tensor.transpose(back[:, b, w, :], by_pair[:, b, w, :], ident[:])
            nc.scalar.copy(
                out=x_grouped[c][:].rearrange("p (b j w) -> p b j w", j=P, w=2),
                in_=back[:].rearrange("p b w j -> p b j w"),
            )
            js = slice(QUARTER * c, QUARTER * (c + 1))
            nc.vector.quantize_mx(
                out=x_codes[:, js].bitcast(FP8X4), scales=x_plane[:, js], in_=x_grouped[c][:].bitcast(BF16)
            )

        def added_on_vector(u, start):
            return u == 0 and start > 0

        def second_stage(u, start, count):
            js = slice(start, start + count)
            ns = slice(P * u, P * (u + 1))
            b_ps = psum.tile([P, count], F32, name="b_ps", tag="product", bufs=PRODUCT_BANKS)
            nc.tensor.matmul_mx(
                out=b_ps[:], lhsT=w3_codes[:, ns].bitcast(FP8X4), lhsT_scale=w3_plane[:, ns],
                rhs=x_codes[:, js].bitcast(FP8X4), rhs_scale=x_plane[:, js], start=True, stop=True,
            )
            a_ps = psum.tile([P, count], F32, name="a_ps", tag="product", bufs=PRODUCT_BANKS)
            nc.tensor.matmul_mx(
                out=a_ps[:], lhsT=w4_codes[:, 2 * P * u : 2 * P * (u + 1)].bitcast(FP4X4),
                lhsT_scale=w4_plane[:, ns], rhs=x_codes[:, js].bitcast(FP8X4), rhs_scale=x_plane[:, js],
                start=True, stop=True,
            )
            nc.scalar.activation(out=gate[:, u, js], in_=a_ps[:], func=ACT.Silu)
            nc.vector.tensor_tensor(prod[:, u, js], b_ps[:], die(u, start, count), MULT)
            if added_on_vector(u, start):
                nc.vector.tensor_tensor(prod[:, u, js], prod[:, u, js], gate[:, u, js], ADD)
                return
            summed = psum.tile([P, count], F32, name="summed", tag="summed")
            for b0 in range(0, count, P):
                bs = slice(start + b0, start + b0 + P)
                nc.tensor.matmul(summed[:, b0 : b0 + P], prod[:, u, bs], ident[:], start=True, stop=False, is_transpose=True)
                nc.tensor.matmul(summed[:, b0 : b0 + P], gate[:, u, bs], ident[:], start=False, stop=True, is_transpose=True)
            nc.scalar.copy(out=gate[:, u, js], in_=summed[:])

        def put_result(u, start, count):
            js = slice(start, start + count)
            if not added_on_vector(u, start):
                y_ps = psum.tile([P, count], F32, name="y_ps", tag="y_ps")
                for b0 in range(0, count, P):
                    nc.tensor.transpose(y_ps[:, b0 : b0 + P], gate[:, u, start + b0 : start + b0 + P], ident[:])
                nc.scalar.copy(out=prod[:, u, js], in_=y_ps[:])
            nc.vector.tensor_tensor(
                catalogue[u][:].indirect(entries(idx4, start, count)), prod[:, u, js], wgo_sb[:, js], MULT
            )

        for c, turn_bank in ((0, "turned"), (1, "summed")):
            buffer = keep.tile([P, HALF], F32, name="shifted%d" % c)[:]
            for u in range(ROW_TILES):
                recall(u, QUARTER * c, QUARTER)
                shift(u, c, buffer)
            quantise_x(c, buffer, stage[c][:], turn_bank)
        nc.vector.quantize_mx(out=w3_codes[:].bitcast(FP8X4), scales=w3_plane[:], in_=w3_bf[:])
        for u in range(ROW_TILES - 1):
            recall(u, HALF, HALF)

        for u in range(ROW_TILES):
            second_stage(u, 0, QUARTER)
        recall(ROW_TILES - 1, HALF, HALF)
        for u in range(ROW_TILES):
            put_result(u, 0, QUARTER)
        for u in range(ROW_TILES):
            second_stage(u, QUARTER, QUARTER)
        for c in range(2, 4):
            for u in range(ROW_TILES):
                shift(u, c, stage[(c + 1) % 2][:])
            quantise_x(c, stage[(c + 1) % 2][:], stage[c % 2][:], "turned")
        for u in range(ROW_TILES):
            put_result(u, QUARTER, QUARTER)

        for u in range(ROW_TILES):
            second_stage(u, HALF, HALF)
        for u in range(ROW_TILES):
            put_result(u, HALF, HALF)
            nc.sync.dma_start(out[P * u : P * (u + 1), :], catalogue[u][:])
